import numpy as np
import ml_dtypes


def mxq(x, axis, fmt="e4m3"):
    dtype, down = {"e4m3": (ml_dtypes.float8_e4m3fn, 7), "e5m2": (ml_dtypes.float8_e5m2, 14)}[fmt]
    v = np.moveaxis(np.asarray(x, np.float32).astype(ml_dtypes.bfloat16).astype(np.float64), axis, -1)
    blocks = v.reshape(v.shape[:-1] + (-1, 32))
    amax = np.abs(blocks).max(-1, keepdims=True)
    byte = np.maximum(np.where(amax > 0, np.frexp(amax)[1] - 1 + 127, 0) - down, 1)
    scale = np.exp2(byte - 127.0)
    codes = (blocks / scale).astype(np.float32).astype(dtype).astype(np.float64)
    return np.moveaxis((codes * scale).reshape(v.shape), -1, axis)


WIDE = False


def mx_kscale(k):
    if not WIDE:
        return np.ones(k)
    levels = np.array([10, -10, 5, -5, 0])
    if k % 512:
        return np.exp2(np.random.permutation(np.resize(levels, k // 32))).repeat(32)
    a = np.empty((k // 512, 16))
    for p in range(k // 512):
        a[p, :8] = np.random.permutation(np.resize(levels, 8))
        for g in range(8):
            far = levels[np.abs(levels - a[p, g]) >= 10]
            a[p, g + 8] = far[np.random.randint(len(far))]
    return np.exp2(a.ravel()).repeat(32)


def f64(x):
    return np.asarray(x).astype(np.float64)


def striped8(idx):
    return np.asarray(idx).reshape(8, -1, 16).transpose(0, 2, 1).reshape(128, -1).astype(np.uint16)


def unstriped8(offs):
    return offs.reshape(8, 16, -1).transpose(0, 2, 1).reshape(8, -1).astype(np.int64)


def pick8(x, idx, run):
    r = np.arange(len(x))
    return x[r[:, None], idx[r % (8 * run) // run]]


E2M1 = np.array([0.0, 0.5, 1.0, 1.5, 2.0, 3.0, 4.0, 6.0, -0.0, -0.5, -1.0, -1.5, -2.0, -3.0, -4.0, -6.0])


def pack_weight(w, fmt):
    k, n = w.shape
    w = f64(np.asarray(w, np.float32).astype(ml_dtypes.bfloat16)).reshape(k // 32, 32, n)
    amax = np.abs(w).max(1)
    if fmt == "e4m3":
        byte = np.frexp(amax)[1] - 1 + 127 - 7
    else:
        mant, ex = np.frexp(amax / 6.0)
        byte = np.where(mant > 0.5, ex, ex - 1) + 127
    byte = np.clip(np.where(amax > 0, byte, 1), 1, 254)
    scaled = (w * np.exp2(127.0 - byte)[:, None, :]).reshape(k, n).astype(np.float32)
    by_word = np.ascontiguousarray(scaled.reshape(k // 512, 128, 4, n).transpose(0, 1, 3, 2))
    if fmt == "e4m3":
        words = by_word.astype(ml_dtypes.float8_e4m3fn).view(np.uint8)
    else:
        c = by_word.astype(ml_dtypes.float4_e2m1fn).view(np.uint8) & 0xF
        words = (c[..., 0::2] | (c[..., 1::2] << 4)).reshape(k // 512, 128, 2 * n)
    return np.ascontiguousarray(words), np.ascontiguousarray(byte.astype(np.uint8).reshape(k // 512, 16, n))


def unpack_weight(words, scales, fmt):
    g, _, n = scales.shape
    words = np.ascontiguousarray(words).reshape(g, 128, n, -1)
    if fmt == "e4m3":
        vals = words.view(ml_dtypes.float8_e4m3fn).astype(np.float64)
    else:
        nib = np.empty((g, 128, n, 4), np.uint8)
        nib[..., 0::2] = words & 0xF
        nib[..., 1::2] = words >> 4
        vals = E2M1[nib]
    vals = vals * np.repeat(np.exp2(scales.astype(np.float64) - 127.0), 8, axis=1)[..., None]
    return vals.transpose(0, 1, 3, 2).reshape(g * 512, n)


def softplus(v):
    return np.log(1.0 + np.exp(v))


D, T, I, Q = 512, 1024, 512, 128


def setup_inputs():
    n = np.random.standard_normal
    idx = np.stack([np.random.permutation(T)[:I] for _ in range(8)])
    idx2 = np.stack([np.random.permutation(T)[:I] for _ in range(8)])
    idx3 = np.stack([np.random.permutation(T)[:I] for _ in range(8)])
    fd = mx_kscale(D)
    keysp = pack_weight(n((D, T)) / fd[:, None], "e4m3")
    return {
        "query": (n((D, Q)) * 0.9 / np.sqrt(D) * fd[:, None]).astype(np.float32),
        "query2": (n((D, Q)) * 0.9 / np.sqrt(D) * fd[:, None]).astype(np.float32),
        "keys_words": keysp[0],
        "keys_scales": keysp[1],
        "lam": (np.random.uniform(0.6, 1.2, (Q, 1))).astype(np.float32),
        "old": (1.0 * n((Q, T))).astype(np.float32),
        "offs": striped8(idx),
        "offs2": striped8(idx2),
        "offs3": striped8(idx3),
    }


def reference(query, query2, keys_words, keys_scales, lam, old, offs, offs2, offs3):
    idx = unstriped8(offs)
    idx2 = unstriped8(offs2)
    idx3 = unstriped8(offs3)
    keysu = unpack_weight(keys_words, keys_scales, "e4m3")
    queryq = mxq(f64(query), 0, "e4m3")
    a = queryq.T @ keysu
    query2q = mxq(f64(query2), 0, "e4m3")
    b = query2q.T @ keysu
    w = pick8(a, idx, 16) / (softplus(pick8(b, idx2, 16)) + 0.5) * f64(lam)
    f1 = np.zeros((Q, T))
    f1[np.arange(Q)[:, None], idx3[np.arange(Q) % 128 // 16]] = w
    y = f64(old) + f1
    return y

@@ -1,0 +1,166 @@
+import math
+from contextlib import ExitStack
+
+import concourse.mybir as mybir
+
+D, T, SLOTS, Q = 512, 1024, 512, 128
+FLOPS = 2 * 2 * D * T * Q
+
+F32 = mybir.dt.float32
+BF16 = mybir.dt.bfloat16
+I32 = mybir.dt.int32
+U32 = mybir.dt.uint32
+U16 = mybir.dt.uint16
+U8 = mybir.dt.uint8
+FP8X4 = mybir.dt.float8_e4m3fn_x4
+ALU = mybir.AluOpType
+ACT = mybir.ActivationFunctionType
+
+P = 128
+HALF = T // 2
+QUARTER = T // 4
+ROOT_E = math.exp(0.5)
+EXP_CAP = 2.0 ** 60
+
+DIRECT = slice(0, 128)
+LOG_PIECES = (slice(320, 512), slice(128, 320))
+HEAD = slice(0, 256)
+TAIL = slice(256, 512)
+FIRST_EXP = slice(128, 256)
+STORE_COLS = 256
+
+
+def list_columns(piece):
+    return slice(piece.start // 16, piece.stop // 16)
+
+
+def tile_attend_worthfor_lean_putold_heads_kernel(
+    tc, query, query2, keys_words, keys_scales, lam, old, offs, offs2, offs3, out
+):
+    nc = tc.nc
+    with ExitStack() as ctx:
+        sb = ctx.enter_context(tc.tile_pool(name="sb", bufs=1))
+        ps = ctx.enter_context(tc.psum_pool(name="ps", bufs=1))
+
+        key_scale = sb.tile([P, T], U8, name="key_scale", align_bytes=64)
+        nc.gpsimd.memset(key_scale[:].bitcast(U32), 0)
+        placed = sb.tile([P, T], F32, name="placed")
+        nc.vector.memset(placed[:], 0.0)
+
+        raw = {}
+        for name, src in (("q2", query2), ("q1", query)):
+            raw[name] = sb.tile([P, 4, Q], F32, name="raw_" + name)
+            nc.sync.dma_start(out=raw[name][:], in_=src.rearrange("(p j) q -> p j q", j=4))
+            if name == "q2":
+                for g in range(4):
+                    nc.sync.dma_start(
+                        out=key_scale[32 * g : 32 * g + 4, :].bitcast(I32),
+                        in_=keys_scales[0, 4 * g : 4 * g + 4, :].bitcast(I32),
+                    )
+        words = keys_words[0].rearrange("p n t -> p (n t)")
+        key_code = []
+        for h in range(2):
+            kc = sb.tile([P, HALF], U32, name="key_code%d" % h, align_bytes=64)
+            nc.sync.dma_start(
+                out=kc[:].bitcast(I32), in_=words[:, 4 * HALF * h : 4 * HALF * (h + 1)].bitcast(I32)
+            )
+            key_code.append(kc)
+        list_b = sb.tile([P, SLOTS // 16], U16, name="list_b")
+        nc.sync.dma_start(list_b[:], offs2)
+        list_a = sb.tile([P, SLOTS // 16], U16, name="list_a")
+        nc.sync.dma_start(list_a[:], offs)
+        lam_col = sb.tile([P, 1], F32, name="lam_col")
+        nc.sync.dma_start(out=lam_col[:], in_=lam)
+        list_put = sb.tile([P, SLOTS // 16], U16, name="list_put")
+        nc.sync.dma_start(list_put[:], offs3)
+        old_sb = sb.tile([P, T], F32, name="old_sb")
+        nc.sync.dma_start(out=old_sb[:], in_=old)
+
+
+        code = {}
+        scale = {}
+        for name in ("q2", "q1"):
+            woven = sb.tile([P, Q, 4], BF16, name="woven_" + name, align_bytes=64)
+            if name == "q2":
+                nc.vector.tensor_copy(out=woven[:], in_=raw[name][:].rearrange("p j q -> p q j"))
+            else:
+                nc.scalar.activation(out=woven[:], in_=raw[name][:].rearrange("p j q -> p q j"), func=ACT.Copy)
+            code[name] = sb.tile([P, Q], U32, name="code_" + name, align_bytes=64)
+            scale[name] = sb.tile([P, Q], U8, name="scale_" + name, align_bytes=64)
+            nc.vector.quantize_mx(
+                out=code[name][:].bitcast(FP8X4),
+                scales=scale[name][:],
+                in_=woven[:].rearrange("p q j -> p (q j)"),
+            )
+
+        def product(name, t0, width):
+            bank = ps.tile([P, width], F32, name="bank_%s_%d" % (name, t0))
+            h, c0 = divmod(t0, HALF)
+            nc.tensor.matmul_mx(
+                out=bank[:],
+                lhsT=code[name][:].bitcast(FP8X4),
+                lhsT_scale=scale[name][:],
+                rhs=key_code[h][:, c0 : c0 + width].bitcast(FP8X4),
+                rhs_scale=key_scale[:, t0 : t0 + width],
+                start=True,
+                stop=True,
+            )
+            return bank
+
+        b_sb = sb.tile([P, T], F32, name="b_sb")
+        a_sb = sb.tile([P, T], F32, name="a_sb")
+        nc.scalar.copy(out=b_sb[:, 0:HALF], in_=product("q2", 0, HALF)[:])
+        nc.scalar.copy(out=b_sb[:, HALF : HALF + QUARTER], in_=product("q2", HALF, QUARTER)[:])
+        nc.vector.tensor_copy(out=b_sb[:, HALF + QUARTER : T], in_=product("q2", HALF + QUARTER, QUARTER)[:])
+        a_banks = [product("q1", 0, HALF), product("q1", HALF, HALF)]
+
+        e = sb.tile([P, SLOTS], F32, name="e")
+        nc.scalar.activation(out=e[:], in_=b_sb[:].indirect(list_b[:]), func=ACT.Exp)
+        x = sb.tile([P, SLOTS], F32, name="x")
+        nc.vector.tensor_copy(out=x[:], in_=b_sb[:].indirect(list_b[:]))
+        nc.vector.tensor_copy(out=a_sb[:, 0:HALF], in_=a_banks[0][:])
+        capped = sb.tile([P, SLOTS], F32, name="capped")
+        nc.vector.tensor_scalar(out=capped[:], in0=e[:], scalar1=EXP_CAP, scalar2=None, op0=ALU.min)
+        nc.vector.tensor_copy(out=a_sb[:, HALF:T], in_=a_banks[1][:])
+
+        soft = sb.tile([P, SLOTS], F32, name="soft")
+        den = sb.tile([P, SLOTS], F32, name="den")
+        log_den = sb.tile([P, SLOTS], F32, name="log_den")
+        inv = sb.tile([P, SLOTS], F32, name="inv")
+        numer = sb.tile([P, SLOTS], F32, name="numer")
+
+        def put(piece):
+            nc.vector.tensor_tensor(
+                out=placed[:].indirect(list_put[:, list_columns(piece)]),
+                in0=numer[:, piece],
+                in1=inv[:, piece],
+                op=ALU.mult,
+            )
+
+        def times_lam(piece, picked):
+            nc.vector.tensor_scalar(out=numer[:, piece], in0=picked, scalar1=lam_col[:], scalar2=None, op0=ALU.mult)
+
+        for piece in LOG_PIECES + (DIRECT,):
+            nc.scalar.activation(out=soft[:, piece], in_=capped[:, piece], func=ACT.Ln, scale=ROOT_E, bias=ROOT_E)
+            nc.vector.scalar_tensor_tensor(
+                out=den[:, piece], in0=x[:, piece], scalar=0.5, in1=soft[:, piece], op0=ALU.add, op1=ALU.max
+            )
+        for piece in LOG_PIECES:
+            nc.scalar.activation(out=log_den[:, piece], in_=den[:, piece], func=ACT.Ln)
+        nc.vector.tensor_copy(out=soft[:, TAIL], in_=a_sb[:].indirect(list_a[:, list_columns(HEAD)]))
+        nc.vector.reciprocal(out=inv[:, DIRECT], in_=den[:, DIRECT])
+        times_lam(HEAD, soft[:, TAIL])
+        put(DIRECT)
+        for piece in (FIRST_EXP, TAIL):
+            nc.scalar.activation(out=inv[:, piece], in_=log_den[:, piece], func=ACT.Exp, scale=-1.0)
+        nc.scalar.activation(out=log_den[:, HEAD], in_=a_sb[:].indirect(list_a[:, list_columns(TAIL)]), func=ACT.Copy)
+        put(FIRST_EXP)
+        times_lam(TAIL, log_den[:, HEAD])
+        put(TAIL)
+
+        for j, t0 in enumerate(range(0, T, STORE_COLS)):
+            cols = slice(t0, t0 + STORE_COLS)
+            total = sb.tile([P, STORE_COLS], F32, name="total%d" % j)
+            nc.vector.tensor_tensor(out=total[:], in0=placed[:, cols], in1=old_sb[:, cols], op=ALU.add)
+            queue = nc.sync if j % 2 == 0 else nc.scalar
+            queue.dma_start(out=out[:, cols], in_=total[:])

@@ -20,13 +20,13 @@ P = 128
 HALF = T // 2
 QUARTER = T // 4
 ROOT_E = math.exp(0.5)
-EXP_CAP = 2.0 ** 60
+EXP_CAP = 40.0
 
 DIRECT = slice(0, 128)
 LOG_PIECES = (slice(320, 512), slice(128, 320))
 HEAD = slice(0, 256)
 TAIL = slice(256, 512)
-FIRST_EXP = slice(128, 256)
+BY_LOG = slice(128, 512)
 STORE_COLS = 256
 
 
@@ -43,7 +43,7 @@ def tile_attend_worthfor_lean_putold_heads_kernel(
         ps = ctx.enter_context(tc.psum_pool(name="ps", bufs=1))
 
         key_scale = sb.tile([P, T], U8, name="key_scale", align_bytes=64)
-        nc.gpsimd.memset(key_scale[:].bitcast(U32), 0)
+        nc.vector.memset(key_scale[:].bitcast(U32), 0)
         placed = sb.tile([P, T], F32, name="placed")
         nc.vector.memset(placed[:], 0.0)
 
@@ -107,20 +107,21 @@ def tile_attend_worthfor_lean_putold_heads_kernel(
             )
             return bank
 
-        b_sb = sb.tile([P, T], F32, name="b_sb")
-        a_sb = sb.tile([P, T], F32, name="a_sb")
+        b_sb = sb.tile([P, T], F32, name="b_sb", tag="scores")
         nc.scalar.copy(out=b_sb[:, 0:HALF], in_=product("q2", 0, HALF)[:])
         nc.scalar.copy(out=b_sb[:, HALF : HALF + QUARTER], in_=product("q2", HALF, QUARTER)[:])
         nc.vector.tensor_copy(out=b_sb[:, HALF + QUARTER : T], in_=product("q2", HALF + QUARTER, QUARTER)[:])
         a_banks = [product("q1", 0, HALF), product("q1", HALF, HALF)]
 
-        e = sb.tile([P, SLOTS], F32, name="e")
-        nc.scalar.activation(out=e[:], in_=b_sb[:].indirect(list_b[:]), func=ACT.Exp)
         x = sb.tile([P, SLOTS], F32, name="x")
-        nc.vector.tensor_copy(out=x[:], in_=b_sb[:].indirect(list_b[:]))
-        nc.vector.tensor_copy(out=a_sb[:, 0:HALF], in_=a_banks[0][:])
+        nc.vector.tensor_copy(out=x[:, HEAD], in_=b_sb[:].indirect(list_b[:, list_columns(HEAD)]))
+        nc.scalar.activation(out=x[:, TAIL], in_=b_sb[:].indirect(list_b[:, list_columns(TAIL)]), func=ACT.Copy)
         capped = sb.tile([P, SLOTS], F32, name="capped")
-        nc.vector.tensor_scalar(out=capped[:], in0=e[:], scalar1=EXP_CAP, scalar2=None, op0=ALU.min)
+        e = sb.tile([P, SLOTS], F32, name="e")
+        nc.vector.tensor_scalar(out=capped[:], in0=x[:], scalar1=EXP_CAP, scalar2=None, op0=ALU.min)
+        a_sb = sb.tile([P, T], F32, name="a_sb", tag="scores")
+        nc.scalar.copy(out=a_sb[:, 0:HALF], in_=a_banks[0][:])
+        nc.scalar.activation(out=e[:], in_=capped[:], func=ACT.Exp)
         nc.vector.tensor_copy(out=a_sb[:, HALF:T], in_=a_banks[1][:])
 
         soft = sb.tile([P, SLOTS], F32, name="soft")
@@ -128,6 +129,7 @@ def tile_attend_worthfor_lean_putold_heads_kernel(
         log_den = sb.tile([P, SLOTS], F32, name="log_den")
         inv = sb.tile([P, SLOTS], F32, name="inv")
         numer = sb.tile([P, SLOTS], F32, name="numer")
+        picked = sb.tile([P, SLOTS], F32, name="picked")
 
         def put(piece):
             nc.vector.tensor_tensor(
@@ -137,26 +139,19 @@ def tile_attend_worthfor_lean_putold_heads_kernel(
                 op=ALU.mult,
             )
 
-        def times_lam(piece, picked):
-            nc.vector.tensor_scalar(out=numer[:, piece], in0=picked, scalar1=lam_col[:], scalar2=None, op0=ALU.mult)
-
+        nc.vector.tensor_copy(out=picked[:], in_=a_sb[:].indirect(list_a[:]))
+        nc.vector.tensor_scalar(out=numer[:], in0=picked[:], scalar1=lam_col[:], scalar2=None, op0=ALU.mult)
         for piece in LOG_PIECES + (DIRECT,):
-            nc.scalar.activation(out=soft[:, piece], in_=capped[:, piece], func=ACT.Ln, scale=ROOT_E, bias=ROOT_E)
+            nc.scalar.activation(out=soft[:, piece], in_=e[:, piece], func=ACT.Ln, scale=ROOT_E, bias=ROOT_E)
             nc.vector.scalar_tensor_tensor(
                 out=den[:, piece], in0=x[:, piece], scalar=0.5, in1=soft[:, piece], op0=ALU.add, op1=ALU.max
             )
         for piece in LOG_PIECES:
             nc.scalar.activation(out=log_den[:, piece], in_=den[:, piece], func=ACT.Ln)
-        nc.vector.tensor_copy(out=soft[:, TAIL], in_=a_sb[:].indirect(list_a[:, list_columns(HEAD)]))
         nc.vector.reciprocal(out=inv[:, DIRECT], in_=den[:, DIRECT])
-        times_lam(HEAD, soft[:, TAIL])
         put(DIRECT)
-        for piece in (FIRST_EXP, TAIL):
-            nc.scalar.activation(out=inv[:, piece], in_=log_den[:, piece], func=ACT.Exp, scale=-1.0)
-        nc.scalar.activation(out=log_den[:, HEAD], in_=a_sb[:].indirect(list_a[:, list_columns(TAIL)]), func=ACT.Copy)
-        put(FIRST_EXP)
-        times_lam(TAIL, log_den[:, HEAD])
-        put(TAIL)
+        nc.scalar.activation(out=inv[:, BY_LOG], in_=log_den[:, BY_LOG], func=ACT.Exp, scale=-1.0)
+        put(BY_LOG)
 
         for j, t0 in enumerate(range(0, T, STORE_COLS)):
             cols = slice(t0, t0 + STORE_COLS)

@@ -20,13 +20,13 @@ P = 128
 HALF = T // 2
 QUARTER = T // 4
 ROOT_E = math.exp(0.5)
-EXP_CAP = 40.0
+DEN_CAP = 40.5
 
-DIRECT = slice(0, 128)
-LOG_PIECES = (slice(320, 512), slice(128, 320))
+DIRECT = slice(384, 512)
+LOG_PIECES = (slice(0, 192), slice(192, 384))
 HEAD = slice(0, 256)
 TAIL = slice(256, 512)
-BY_LOG = slice(128, 512)
+BY_LOG = slice(0, 384)
 STORE_COLS = 256
 
 
@@ -80,7 +80,8 @@ def tile_attend_worthfor_lean_putold_heads_kernel(
         code = {}
         scale = {}
         for name in ("q2", "q1"):
-            woven = sb.tile([P, Q, 4], BF16, name="woven_" + name, align_bytes=64)
+            tag = "scores" if name == "q1" else "woven_q2"
+            woven = sb.tile([P, Q, 4], BF16, name="woven_" + name, tag=tag, align_bytes=64)
             if name == "q2":
                 nc.vector.tensor_copy(out=woven[:], in_=raw[name][:].rearrange("p j q -> p q j"))
             else:
@@ -107,28 +108,34 @@ def tile_attend_worthfor_lean_putold_heads_kernel(
             )
             return bank
 
-        b_sb = sb.tile([P, T], F32, name="b_sb", tag="scores")
+        b_sb = sb.tile([P, T], F32, name="b_sb", tag="scores", align_bytes=64)
         nc.scalar.copy(out=b_sb[:, 0:HALF], in_=product("q2", 0, HALF)[:])
         nc.scalar.copy(out=b_sb[:, HALF : HALF + QUARTER], in_=product("q2", HALF, QUARTER)[:])
         nc.vector.tensor_copy(out=b_sb[:, HALF + QUARTER : T], in_=product("q2", HALF + QUARTER, QUARTER)[:])
         a_banks = [product("q1", 0, HALF), product("q1", HALF, HALF)]
 
         x = sb.tile([P, SLOTS], F32, name="x")
-        nc.vector.tensor_copy(out=x[:, HEAD], in_=b_sb[:].indirect(list_b[:, list_columns(HEAD)]))
-        nc.scalar.activation(out=x[:, TAIL], in_=b_sb[:].indirect(list_b[:, list_columns(TAIL)]), func=ACT.Copy)
-        capped = sb.tile([P, SLOTS], F32, name="capped")
+        nc.vector.tensor_scalar(
+            out=x[:, HEAD],
+            in0=b_sb[:].indirect(list_b[:, list_columns(HEAD)]),
+            scalar1=1.0,
+            scalar2=0.5,
+            op0=ALU.mult,
+            op1=ALU.add,
+        )
+        nc.scalar.activation(
+            out=x[:, TAIL], in_=b_sb[:].indirect(list_b[:, list_columns(TAIL)]), func=ACT.Copy, bias=0.5
+        )
         e = sb.tile([P, SLOTS], F32, name="e")
-        nc.vector.tensor_scalar(out=capped[:], in0=x[:], scalar1=EXP_CAP, scalar2=None, op0=ALU.min)
-        a_sb = sb.tile([P, T], F32, name="a_sb", tag="scores")
-        nc.scalar.copy(out=a_sb[:, 0:HALF], in_=a_banks[0][:])
-        nc.scalar.activation(out=e[:], in_=capped[:], func=ACT.Exp)
+        for piece in (HEAD, TAIL):
+            nc.scalar.activation(out=e[:, piece], in_=x[:, piece], func=ACT.Exp)
+        a_sb = sb.tile([P, T], F32, name="a_sb", tag="scores", align_bytes=64)
+        nc.vector.tensor_copy(out=a_sb[:, 0:HALF], in_=a_banks[0][:])
         nc.vector.tensor_copy(out=a_sb[:, HALF:T], in_=a_banks[1][:])
 
-        soft = sb.tile([P, SLOTS], F32, name="soft")
-        den = sb.tile([P, SLOTS], F32, name="den")
+        soft = sb.tile([P, SLOTS], F32, name="soft", tag="factor")
         log_den = sb.tile([P, SLOTS], F32, name="log_den")
         inv = sb.tile([P, SLOTS], F32, name="inv")
-        numer = sb.tile([P, SLOTS], F32, name="numer")
         picked = sb.tile([P, SLOTS], F32, name="picked")
 
         def put(piece):
@@ -140,17 +147,22 @@ def tile_attend_worthfor_lean_putold_heads_kernel(
             )
 
         nc.vector.tensor_copy(out=picked[:], in_=a_sb[:].indirect(list_a[:]))
-        nc.vector.tensor_scalar(out=numer[:], in0=picked[:], scalar1=lam_col[:], scalar2=None, op0=ALU.mult)
+        den = sb.tile([P, SLOTS], F32, name="den", tag="scores", align_bytes=64)
         for piece in LOG_PIECES + (DIRECT,):
-            nc.scalar.activation(out=soft[:, piece], in_=e[:, piece], func=ACT.Ln, scale=ROOT_E, bias=ROOT_E)
+            nc.scalar.activation(out=soft[:, piece], in_=e[:, piece], func=ACT.Ln, bias=ROOT_E)
             nc.vector.scalar_tensor_tensor(
-                out=den[:, piece], in0=x[:, piece], scalar=0.5, in1=soft[:, piece], op0=ALU.add, op1=ALU.max
+                out=den[:, piece], in0=soft[:, piece], scalar=DEN_CAP, in1=x[:, piece], op0=ALU.min, op1=ALU.max
             )
         for piece in LOG_PIECES:
             nc.scalar.activation(out=log_den[:, piece], in_=den[:, piece], func=ACT.Ln)
         nc.vector.reciprocal(out=inv[:, DIRECT], in_=den[:, DIRECT])
+        numer = sb.tile([P, SLOTS], F32, name="numer", tag="factor")
+        nc.gpsimd.tensor_scalar(
+            out=numer[:], in0=picked[:], scalar1=lam_col[:], scalar2=0.0, op0=ALU.mult, op1=ALU.add
+        )
         put(DIRECT)
-        nc.scalar.activation(out=inv[:, BY_LOG], in_=log_den[:, BY_LOG], func=ACT.Exp, scale=-1.0)
+        for piece in LOG_PIECES:
+            nc.scalar.activation(out=inv[:, piece], in_=log_den[:, piece], func=ACT.Exp, scale=-1.0)
         put(BY_LOG)
 
         for j, t0 in enumerate(range(0, T, STORE_COLS)):

@@ -22,11 +22,11 @@ QUARTER = T // 4
 ROOT_E = math.exp(0.5)
 DEN_CAP = 40.5
 
-DIRECT = slice(384, 512)
-LOG_PIECES = (slice(0, 192), slice(192, 384))
+DIRECT = slice(352, 512)
+LOG_PIECES = (slice(0, 176), slice(176, 352))
 HEAD = slice(0, 256)
 TAIL = slice(256, 512)
-BY_LOG = slice(0, 384)
+BY_LOG = slice(0, 352)
 STORE_COLS = 256
 
 
@@ -48,15 +48,17 @@ def tile_attend_worthfor_lean_putold_heads_kernel(
         nc.vector.memset(placed[:], 0.0)
 
         raw = {}
-        for name, src in (("q2", query2), ("q1", query)):
+
+        def load_query(name, src):
             raw[name] = sb.tile([P, 4, Q], F32, name="raw_" + name)
             nc.sync.dma_start(out=raw[name][:], in_=src.rearrange("(p j) q -> p j q", j=4))
-            if name == "q2":
-                for g in range(4):
-                    nc.sync.dma_start(
-                        out=key_scale[32 * g : 32 * g + 4, :].bitcast(I32),
-                        in_=keys_scales[0, 4 * g : 4 * g + 4, :].bitcast(I32),
-                    )
+
+        load_query("q2", query2)
+        for g in range(4):
+            nc.sync.dma_start(
+                out=key_scale[32 * g : 32 * g + 4, :].bitcast(I32),
+                in_=keys_scales[0, 4 * g : 4 * g + 4, :].bitcast(I32),
+            )
         words = keys_words[0].rearrange("p n t -> p (n t)")
         key_code = []
         for h in range(2):
@@ -65,6 +67,7 @@ def tile_attend_worthfor_lean_putold_heads_kernel(
                 out=kc[:].bitcast(I32), in_=words[:, 4 * HALF * h : 4 * HALF * (h + 1)].bitcast(I32)
             )
             key_code.append(kc)
+        load_query("q1", query)
         list_b = sb.tile([P, SLOTS // 16], U16, name="list_b")
         nc.sync.dma_start(list_b[:], offs2)
         list_a = sb.tile([P, SLOTS // 16], U16, name="list_a")
@@ -79,13 +82,10 @@ def tile_attend_worthfor_lean_putold_heads_kernel(
 
         code = {}
         scale = {}
-        for name in ("q2", "q1"):
-            tag = "scores" if name == "q1" else "woven_q2"
-            woven = sb.tile([P, Q, 4], BF16, name="woven_" + name, tag=tag, align_bytes=64)
-            if name == "q2":
-                nc.vector.tensor_copy(out=woven[:], in_=raw[name][:].rearrange("p j q -> p q j"))
-            else:
-                nc.scalar.activation(out=woven[:], in_=raw[name][:].rearrange("p j q -> p q j"), func=ACT.Copy)
+
+        def quantise(name):
+            woven = sb.tile([P, Q, 4], BF16, name="woven_" + name, align_bytes=64)
+            nc.vector.tensor_copy(out=woven[:], in_=raw[name][:].rearrange("p j q -> p q j"))
             code[name] = sb.tile([P, Q], U32, name="code_" + name, align_bytes=64)
             scale[name] = sb.tile([P, Q], U8, name="scale_" + name, align_bytes=64)
             nc.vector.quantize_mx(
@@ -95,10 +95,10 @@ def tile_attend_worthfor_lean_putold_heads_kernel(
             )
 
         def product(name, t0, width):
-            bank = ps.tile([P, width], F32, name="bank_%s_%d" % (name, t0))
+            bank = ps.tile([P, HALF], F32, name="bank_%s_%d" % (name, t0))
             h, c0 = divmod(t0, HALF)
             nc.tensor.matmul_mx(
-                out=bank[:],
+                out=bank[:, 0:width],
                 lhsT=code[name][:].bitcast(FP8X4),
                 lhsT_scale=scale[name][:],
                 rhs=key_code[h][:, c0 : c0 + width].bitcast(FP8X4),
@@ -106,12 +106,14 @@ def tile_attend_worthfor_lean_putold_heads_kernel(
                 start=True,
                 stop=True,
             )
-            return bank
+            return bank[:, 0:width]
 
+        quantise("q2")
         b_sb = sb.tile([P, T], F32, name="b_sb", tag="scores", align_bytes=64)
-        nc.scalar.copy(out=b_sb[:, 0:HALF], in_=product("q2", 0, HALF)[:])
-        nc.scalar.copy(out=b_sb[:, HALF : HALF + QUARTER], in_=product("q2", HALF, QUARTER)[:])
-        nc.vector.tensor_copy(out=b_sb[:, HALF + QUARTER : T], in_=product("q2", HALF + QUARTER, QUARTER)[:])
+        nc.vector.tensor_copy(out=b_sb[:, 0:QUARTER], in_=product("q2", 0, QUARTER))
+        for t0 in range(QUARTER, T, QUARTER):
+            nc.scalar.activation(out=b_sb[:, t0 : t0 + QUARTER], in_=product("q2", t0, QUARTER), func=ACT.Copy)
+        quantise("q1")
         a_banks = [product("q1", 0, HALF), product("q1", HALF, HALF)]
 
         x = sb.tile([P, SLOTS], F32, name="x")
@@ -127,11 +129,10 @@ def tile_attend_worthfor_lean_putold_heads_kernel(
             out=x[:, TAIL], in_=b_sb[:].indirect(list_b[:, list_columns(TAIL)]), func=ACT.Copy, bias=0.5
         )
         e = sb.tile([P, SLOTS], F32, name="e")
-        for piece in (HEAD, TAIL):
-            nc.scalar.activation(out=e[:, piece], in_=x[:, piece], func=ACT.Exp)
+        nc.scalar.activation(out=e[:], in_=x[:], func=ACT.Exp)
         a_sb = sb.tile([P, T], F32, name="a_sb", tag="scores", align_bytes=64)
-        nc.vector.tensor_copy(out=a_sb[:, 0:HALF], in_=a_banks[0][:])
-        nc.vector.tensor_copy(out=a_sb[:, HALF:T], in_=a_banks[1][:])
+        nc.vector.tensor_copy(out=a_sb[:, 0:HALF], in_=a_banks[0])
+        nc.vector.tensor_copy(out=a_sb[:, HALF:T], in_=a_banks[1])
 
         soft = sb.tile([P, SLOTS], F32, name="soft", tag="factor")
         log_den = sb.tile([P, SLOTS], F32, name="log_den")

import math
from contextlib import ExitStack

import concourse.mybir as mybir

D, T, SLOTS, Q = 512, 1024, 512, 128
FLOPS = 2 * 2 * D * T * Q

F32 = mybir.dt.float32
BF16 = mybir.dt.bfloat16
I32 = mybir.dt.int32
U32 = mybir.dt.uint32
U16 = mybir.dt.uint16
U8 = mybir.dt.uint8
FP8X4 = mybir.dt.float8_e4m3fn_x4
ALU = mybir.AluOpType
ACT = mybir.ActivationFunctionType

P = 128
HALF = T // 2
QUARTER = T // 4
ROOT_E = math.exp(0.5)
DEN_CAP = 40.5

DIRECT = slice(352, 512)
LOG_PIECES = (slice(0, 176), slice(176, 352))
HEAD = slice(0, 256)
TAIL = slice(256, 512)
BY_LOG = slice(0, 352)
STORE_COLS = 256


def list_columns(piece):
    return slice(piece.start // 16, piece.stop // 16)


def tile_attend_worthfor_lean_putold_heads_kernel(
    tc, query, query2, keys_words, keys_scales, lam, old, offs, offs2, offs3, out
):
    nc = tc.nc
    with ExitStack() as ctx:
        sb = ctx.enter_context(tc.tile_pool(name="sb", bufs=1))
        ps = ctx.enter_context(tc.psum_pool(name="ps", bufs=1))

        key_scale = sb.tile([P, T], U8, name="key_scale", align_bytes=64)
        nc.vector.memset(key_scale[:].bitcast(U32), 0)
        placed = sb.tile([P, T], F32, name="placed")
        nc.vector.memset(placed[:], 0.0)

        raw = {}

        def load_query(name, src):
            raw[name] = sb.tile([P, 4, Q], F32, name="raw_" + name)
            nc.sync.dma_start(out=raw[name][:], in_=src.rearrange("(p j) q -> p j q", j=4))

        load_query("q2", query2)
        for g in range(4):
            nc.sync.dma_start(
                out=key_scale[32 * g : 32 * g + 4, :].bitcast(I32),
                in_=keys_scales[0, 4 * g : 4 * g + 4, :].bitcast(I32),
            )
        words = keys_words[0].rearrange("p n t -> p (n t)")
        key_code = []
        for h in range(2):
            kc = sb.tile([P, HALF], U32, name="key_code%d" % h, align_bytes=64)
            nc.sync.dma_start(
                out=kc[:].bitcast(I32), in_=words[:, 4 * HALF * h : 4 * HALF * (h + 1)].bitcast(I32)
            )
            key_code.append(kc)
        load_query("q1", query)
        list_b = sb.tile([P, SLOTS // 16], U16, name="list_b")
        nc.sync.dma_start(list_b[:], offs2)
        list_a = sb.tile([P, SLOTS // 16], U16, name="list_a")
        nc.sync.dma_start(list_a[:], offs)
        lam_col = sb.tile([P, 1], F32, name="lam_col")
        nc.sync.dma_start(out=lam_col[:], in_=lam)
        list_put = sb.tile([P, SLOTS // 16], U16, name="list_put")
        nc.sync.dma_start(list_put[:], offs3)
        old_sb = sb.tile([P, T], F32, name="old_sb")
        nc.sync.dma_start(out=old_sb[:], in_=old)


        code = {}
        scale = {}

        def quantise(name):
            woven = sb.tile([P, Q, 4], BF16, name="woven_" + name, align_bytes=64)
            nc.vector.tensor_copy(out=woven[:], in_=raw[name][:].rearrange("p j q -> p q j"))
            code[name] = sb.tile([P, Q], U32, name="code_" + name, align_bytes=64)
            scale[name] = sb.tile([P, Q], U8, name="scale_" + name, align_bytes=64)
            nc.vector.quantize_mx(
                out=code[name][:].bitcast(FP8X4),
                scales=scale[name][:],
                in_=woven[:].rearrange("p q j -> p (q j)"),
            )

        def product(name, t0, width):
            bank = ps.tile([P, HALF], F32, name="bank_%s_%d" % (name, t0))
            h, c0 = divmod(t0, HALF)
            nc.tensor.matmul_mx(
                out=bank[:, 0:width],
                lhsT=code[name][:].bitcast(FP8X4),
                lhsT_scale=scale[name][:],
                rhs=key_code[h][:, c0 : c0 + width].bitcast(FP8X4),
                rhs_scale=key_scale[:, t0 : t0 + width],
                start=True,
                stop=True,
            )
            return bank[:, 0:width]

        quantise("q2")
        b_sb = sb.tile([P, T], F32, name="b_sb", tag="scores", align_bytes=64)
        nc.vector.tensor_copy(out=b_sb[:, 0:QUARTER], in_=product("q2", 0, QUARTER))
        for t0 in range(QUARTER, T, QUARTER):
            nc.scalar.activation(out=b_sb[:, t0 : t0 + QUARTER], in_=product("q2", t0, QUARTER), func=ACT.Copy)
        quantise("q1")
        a_banks = [product("q1", 0, HALF), product("q1", HALF, HALF)]

        x = sb.tile([P, SLOTS], F32, name="x")
        nc.vector.tensor_scalar(
            out=x[:, HEAD],
            in0=b_sb[:].indirect(list_b[:, list_columns(HEAD)]),
            scalar1=1.0,
            scalar2=0.5,
            op0=ALU.mult,
            op1=ALU.add,
        )
        nc.scalar.activation(
            out=x[:, TAIL], in_=b_sb[:].indirect(list_b[:, list_columns(TAIL)]), func=ACT.Copy, bias=0.5
        )
        e = sb.tile([P, SLOTS], F32, name="e")
        nc.scalar.activation(out=e[:], in_=x[:], func=ACT.Exp)
        a_sb = sb.tile([P, T], F32, name="a_sb", tag="scores", align_bytes=64)
        nc.vector.tensor_copy(out=a_sb[:, 0:HALF], in_=a_banks[0])
        nc.vector.tensor_copy(out=a_sb[:, HALF:T], in_=a_banks[1])

        soft = sb.tile([P, SLOTS], F32, name="soft", tag="factor")
        log_den = sb.tile([P, SLOTS], F32, name="log_den")
        inv = sb.tile([P, SLOTS], F32, name="inv")
        picked = sb.tile([P, SLOTS], F32, name="picked")

        def put(piece):
            nc.vector.tensor_tensor(
                out=placed[:].indirect(list_put[:, list_columns(piece)]),
                in0=numer[:, piece],
                in1=inv[:, piece],
                op=ALU.mult,
            )

        nc.vector.tensor_copy(out=picked[:], in_=a_sb[:].indirect(list_a[:]))
        den = sb.tile([P, SLOTS], F32, name="den", tag="scores", align_bytes=64)
        for piece in LOG_PIECES + (DIRECT,):
            nc.scalar.activation(out=soft[:, piece], in_=e[:, piece], func=ACT.Ln, bias=ROOT_E)
            nc.vector.scalar_tensor_tensor(
                out=den[:, piece], in0=soft[:, piece], scalar=DEN_CAP, in1=x[:, piece], op0=ALU.min, op1=ALU.max
            )
        for piece in LOG_PIECES:
            nc.scalar.activation(out=log_den[:, piece], in_=den[:, piece], func=ACT.Ln)
        nc.vector.reciprocal(out=inv[:, DIRECT], in_=den[:, DIRECT])
        numer = sb.tile([P, SLOTS], F32, name="numer", tag="factor")
        nc.gpsimd.tensor_scalar(
            out=numer[:], in0=picked[:], scalar1=lam_col[:], scalar2=0.0, op0=ALU.mult, op1=ALU.add
        )
        put(DIRECT)
        for piece in LOG_PIECES:
            nc.scalar.activation(out=inv[:, piece], in_=log_den[:, piece], func=ACT.Exp, scale=-1.0)
        put(BY_LOG)

        for j, t0 in enumerate(range(0, T, STORE_COLS)):
            cols = slice(t0, t0 + STORE_COLS)
            total = sb.tile([P, STORE_COLS], F32, name="total%d" % j)
            nc.vector.tensor_tensor(out=total[:], in0=placed[:, cols], in1=old_sb[:, cols], op=ALU.add)
            queue = nc.sync if j % 2 == 0 else nc.scalar
            queue.dma_start(out=out[:, cols], in_=total[:])
